import numpy as np
import ml_dtypes


def mxq(x, axis, fmt="e4m3"):
    dtype, down = {"e4m3": (ml_dtypes.float8_e4m3fn, 7), "e5m2": (ml_dtypes.float8_e5m2, 14)}[fmt]
    v = np.moveaxis(np.asarray(x, np.float32).astype(ml_dtypes.bfloat16).astype(np.float64), axis, -1)
    blocks = v.reshape(v.shape[:-1] + (-1, 32))
    amax = np.abs(blocks).max(-1, keepdims=True)
    byte = np.maximum(np.where(amax > 0, np.frexp(amax)[1] - 1 + 127, 0) - down, 1)
    scale = np.exp2(byte - 127.0)
    codes = (blocks / scale).astype(np.float32).astype(dtype).astype(np.float64)
    return np.moveaxis((codes * scale).reshape(v.shape), -1, axis)


WIDE = False


def mx_kscale(k):
    if not WIDE:
        return np.ones(k)
    levels = np.array([10, -10, 5, -5, 0])
    if k % 512:
        return np.exp2(np.random.permutation(np.resize(levels, k // 32))).repeat(32)
    a = np.empty((k // 512, 16))
    for p in range(k // 512):
        a[p, :8] = np.random.permutation(np.resize(levels, 8))
        for g in range(8):
            far = levels[np.abs(levels - a[p, g]) >= 10]
            a[p, g + 8] = far[np.random.randint(len(far))]
    return np.exp2(a.ravel()).repeat(32)


def f64(x):
    return np.asarray(x).astype(np.float64)


def striped8(idx):
    return np.asarray(idx).reshape(8, -1, 16).transpose(0, 2, 1).reshape(128, -1).astype(np.uint16)


def unstriped8(offs):
    return offs.reshape(8, 16, -1).transpose(0, 2, 1).reshape(8, -1).astype(np.int64)


def pick8(x, idx, run):
    r = np.arange(len(x))
    return x[r[:, None], idx[r % (8 * run) // run]]


E2M1 = np.array([0.0, 0.5, 1.0, 1.5, 2.0, 3.0, 4.0, 6.0, -0.0, -0.5, -1.0, -1.5, -2.0, -3.0, -4.0, -6.0])


def pack_weight(w, fmt):
    k, n = w.shape
    w = f64(np.asarray(w, np.float32).astype(ml_dtypes.bfloat16)).reshape(k // 32, 32, n)
    amax = np.abs(w).max(1)
    if fmt == "e4m3":
        byte = np.frexp(amax)[1] - 1 + 127 - 7
    else:
        mant, ex = np.frexp(amax / 6.0)
        byte = np.where(mant > 0.5, ex, ex - 1) + 127
    byte = np.clip(np.where(amax > 0, byte, 1), 1, 254)
    scaled = (w * np.exp2(127.0 - byte)[:, None, :]).reshape(k, n).astype(np.float32)
    by_word = np.ascontiguousarray(scaled.reshape(k // 512, 128, 4, n).transpose(0, 1, 3, 2))
    if fmt == "e4m3":
        words = by_word.astype(ml_dtypes.float8_e4m3fn).view(np.uint8)
    else:
        c = by_word.astype(ml_dtypes.float4_e2m1fn).view(np.uint8) & 0xF
        words = (c[..., 0::2] | (c[..., 1::2] << 4)).reshape(k // 512, 128, 2 * n)
    return np.ascontiguousarray(words), np.ascontiguousarray(byte.astype(np.uint8).reshape(k // 512, 16, n))


def unpack_weight(words, scales, fmt):
    g, _, n = scales.shape
    words = np.ascontiguousarray(words).reshape(g, 128, n, -1)
    if fmt == "e4m3":
        vals = words.view(ml_dtypes.float8_e4m3fn).astype(np.float64)
    else:
        nib = np.empty((g, 128, n, 4), np.uint8)
        nib[..., 0::2] = words & 0xF
        nib[..., 1::2] = words >> 4
        vals = E2M1[nib]
    vals = vals * np.repeat(np.exp2(scales.astype(np.float64) - 127.0), 8, axis=1)[..., None]
    return vals.transpose(0, 1, 3, 2).reshape(g * 512, n)


D, K, T, U, X, I, Q = 512, 512, 1024, 1024, 1024, 512, 128


def setup_inputs():
    n = np.random.standard_normal
    idx = np.stack([np.random.permutation(T)[:I] for _ in range(8)])
    idx2 = np.stack([np.random.permutation(U)[:I] for _ in range(8)])
    idx3 = np.stack([np.random.permutation(X)[:I] for _ in range(8)])
    idx4 = np.stack([np.random.permutation(X)[:I] for _ in range(8)])
    idx5 = np.stack([np.random.permutation(T)[:I] for _ in range(8)])
    idx6 = np.stack([np.random.permutation(T)[:I] for _ in range(8)])
    fd = mx_kscale(D)
    fk = mx_kscale(K)
    wqp = pack_weight(n((D, K)) * 1.0 / np.sqrt(D) * fd[:, None] * fk, "e4m3")
    cachep = pack_weight(n((K, T)) * 1.0 / np.sqrt(K) / fk[:, None], "e2m1")
    draftp = pack_weight(n((K, U)) * 1.0 / np.sqrt(K) / fk[:, None], "e4m3")
    archp = pack_weight(n((D, X)) * 1.0 / np.sqrt(D) * fd[:, None], "e2m1")
    return {
        "states": (n((D, Q)) * 0.95 / fd[:, None]).astype(np.float32),
        "wq_words": wqp[0],
        "wq_scales": wqp[1],
        "cache_words": cachep[0],
        "cache_scales": cachep[1],
        "draft_words": draftp[0],
        "draft_scales": draftp[1],
        "arch_words": archp[0],
        "arch_scales": archp[1],
        "offs": striped8(idx),
        "offs2": striped8(idx2),
        "offs3": striped8(idx3),
        "offs4": striped8(idx4),
        "offs5": striped8(idx5),
        "offs6": striped8(idx6),
    }


def reference(states, wq_words, wq_scales, cache_words, cache_scales, draft_words, draft_scales, arch_words, arch_scales, offs, offs2, offs3, offs4, offs5, offs6):
    idx = unstriped8(offs)
    idx2 = unstriped8(offs2)
    idx3 = unstriped8(offs3)
    idx4 = unstriped8(offs4)
    idx5 = unstriped8(offs5)
    idx6 = unstriped8(offs6)
    wqu = unpack_weight(wq_words, wq_scales, "e4m3")
    cacheu = unpack_weight(cache_words, cache_scales, "e2m1")
    draftu = unpack_weight(draft_words, draft_scales, "e4m3")
    archu = unpack_weight(arch_words, arch_scales, "e2m1")
    statesq = mxq(f64(states), 0, "e4m3")
    qv = wqu.T @ statesq
    qvq = mxq(qv, 0, "e4m3")
    a = qvq.T @ cacheu
    b = qvq.T @ draftu
    c0 = statesq.T @ archu
    w = pick8(a, idx, 16) - pick8(b, idx2, 16)
    cl = np.max(w, axis=1, keepdims=True) * 0.25
    v = np.maximum(w, cl)
    f1 = np.zeros((Q, X))
    f1[np.arange(Q)[:, None], idx3[np.arange(Q) % 128 // 16]] = v
    cc = c0 + f1
    r = pick8(cc, idx4, 16) - w
    f2 = np.zeros((Q, T))
    f2[np.arange(Q)[:, None], idx5[np.arange(Q) % 128 // 16]] = r
    aa = a - f2
    y = np.maximum(pick8(aa, idx6, 16), pick8(b, idx2, 16))
    return y

@@ -1,0 +1,211 @@
+from contextlib import ExitStack
+
+import concourse.mybir as mybir
+
+F32 = mybir.dt.float32
+BF16 = mybir.dt.bfloat16
+I32 = mybir.dt.int32
+U32 = mybir.dt.uint32
+U16 = mybir.dt.uint16
+U8 = mybir.dt.uint8
+FP8X4 = mybir.dt.float8_e4m3fn_x4
+FP4X4 = mybir.dt.float4_e2m1fn_x4
+ALU = mybir.AluOpType
+COPY = mybir.ActivationFunctionType.Copy
+
+P = 128
+PACK = 4
+FEATURES = 512
+ROWS = 128
+TOKENS = 1024
+SLOTS = 512
+BANK = 512
+HALF = SLOTS // 2
+GROUP = 16
+
+FLOPS = 2 * FEATURES * ROWS * (FEATURES + 3 * TOKENS)
+
+
+def tile_attend_overbar_sidethree_kernel(
+    tc, states, wq_words, wq_scales, cache_words, cache_scales, draft_words, draft_scales,
+    arch_words, arch_scales, offs, offs2, offs3, offs4, offs5, offs6, out,
+):
+    nc = tc.nc
+    with ExitStack() as ctx:
+        sb = ctx.enter_context(tc.tile_pool(name="sb", bufs=1))
+        ps = ctx.enter_context(tc.psum_pool(name="ps", bufs=1))
+
+        def scale_tile(engine, name, width, base):
+            t = sb.tile([P, 2 * width], U8, name=name, align_bytes=64)
+            engine.memset(t[base : base + 64, :].bitcast(I32), 0)
+            return t
+
+        def load_scales(queue, t, scales, base, first):
+            rows = scales[0].bitcast(I32).rearrange("(a b j) n -> b j a n", a=2, b=2)
+            for b in range(2):
+                p0 = base + 32 * b + first
+                queue.dma_start(
+                    out=t[p0 : p0 + 4, :].bitcast(I32).rearrange("j (a n) -> j a n", a=2), in_=rows[b]
+                )
+
+        def spread_scales(t, width, base, first):
+            low, high = slice(0, width), slice(width, 2 * width)
+            if base == 0:
+                nc.vector.tensor_copy(out=t[64:128, low].bitcast(I32), in_=t[0:64, high].bitcast(I32))
+                return t[first:P, low]
+            nc.vector.tensor_copy(out=t[0:64, high].bitcast(I32), in_=t[64:128, low].bitcast(I32))
+            return t[first:P, high]
+
+        arch_st = scale_tile(nc.vector, "arch_st", TOKENS, 64)
+        wq_st = sb.tile([P, FEATURES], U8, align_bytes=64)
+        nc.vector.memset(wq_st[:].bitcast(I32), 0)
+        draft_st = scale_tile(nc.gpsimd, "draft_st", TOKENS, 0)
+        cache_st = scale_tile(nc.gpsimd, "cache_st", TOKENS, 0)
+
+        wq_rows = sb.tile([4, 4, FEATURES // 4], I32)
+        nc.sync.dma_start(out=wq_rows[:], in_=wq_scales[0].bitcast(I32).rearrange("(g j) n -> j g n", j=4))
+        raw = sb.tile([P, PACK, ROWS], F32)
+        nc.sync.dma_start(out=raw[:], in_=states.rearrange("(p j) q -> p j q", j=PACK))
+        wq_raw = sb.tile([P, FEATURES], U32, align_bytes=64)
+        nc.sync.dma_start(out=wq_raw[:].bitcast(I32), in_=wq_words[0].rearrange("p n t -> p (n t)").bitcast(I32))
+        load_scales(nc.sync, arch_st, arch_scales, 64, 0)
+        arch_w = sb.tile([P, 2 * TOKENS], U8, align_bytes=64)
+        nc.sync.dma_start(out=arch_w[:].bitcast(I32), in_=arch_words[0].bitcast(I32))
+        load_scales(nc.sync, draft_st, draft_scales, 0, 4)
+        draft_w = sb.tile([P, TOKENS], U32, align_bytes=64, tag="draft_then_f1")
+        nc.sync.dma_start(out=draft_w[:].bitcast(I32), in_=draft_words[0].rearrange("p n t -> p (n t)").bitcast(I32))
+        load_scales(nc.sync, cache_st, cache_scales, 0, 0)
+        cache_w = sb.tile([P, 2 * TOKENS], U8, align_bytes=64)
+        nc.sync.dma_start(out=cache_w[:].bitcast(I32), in_=cache_words[0].bitcast(I32))
+        lists = {}
+        for name, src in (("l2", offs2), ("l1", offs), ("l3", offs3), ("l4", offs4), ("l5", offs5), ("l6", offs6)):
+            lists[name] = sb.tile([P, SLOTS // GROUP], U16, name=name)
+            nc.sync.dma_start(lists[name][:], src)
+
+        def half(name, h):
+            k = HALF // GROUP
+            return lists[name][:, h * k : (h + 1) * k]
+
+
+        for g in range(4):
+            nc.vector.tensor_copy(out=wq_st[32 * g : 32 * g + 4, :].bitcast(I32), in_=wq_rows[:, g, :])
+        grouped = sb.tile([P, ROWS, PACK], BF16, align_bytes=64)
+        wq_sc = sb.tile([P, PACK, P], U8, align_bytes=64)
+        nc.vector.tensor_copy(
+            out=wq_sc[:].rearrange("p t m -> p m t"),
+            in_=wq_st[:].rearrange("p (m t) -> p m t", t=PACK),
+        )
+        woven = grouped[:].rearrange("p (c i) t -> p c t i", i=4)
+        planes = raw[:].rearrange("p t (c i) -> p c t i", i=4)
+        nc.vector.tensor_copy(out=woven[:, 0:16], in_=planes[:, 0:16])
+        nc.scalar.copy(out=woven[:, 16:32], in_=planes[:, 16:32])
+        wq_w = sb.tile([P, PACK, P], U32, align_bytes=64)
+        dealt = wq_w[:].rearrange("p t m -> p m t")
+        undealt = wq_raw[:].rearrange("p (m t) -> p m t", t=PACK)
+        nc.scalar.copy(out=dealt[:, 0:48, :], in_=undealt[:, 0:48, :])
+        nc.vector.tensor_copy(out=dealt[:, 48:P, :].bitcast(I32), in_=undealt[:, 48:P, :].bitcast(I32))
+        s_codes = wq_raw[:, FEATURES - ROWS : FEATURES]
+        s_scales = sb.tile([P, ROWS], U8, align_bytes=64)
+        nc.vector.quantize_mx(
+            out=s_codes.bitcast(FP8X4), scales=s_scales[:], in_=grouped[:].rearrange("p q t -> p (q t)")
+        )
+
+        qv_ps = ps.tile([P, PACK, ROWS], F32)
+        for t in range(PACK):
+            nc.tensor.matmul_mx(
+                out=qv_ps[:, t, :], lhsT=wq_w[:, t, :].bitcast(FP8X4), lhsT_scale=wq_sc[:, t, :],
+                rhs=s_codes.bitcast(FP8X4), rhs_scale=s_scales[:], start=True, stop=True,
+            )
+
+        def score(name, codes, scales, words, plane, fp4):
+            banks = []
+            for h in range(TOKENS // BANK):
+                bank = ps.tile([P, BANK], F32, name=name + str(h))
+                cols = slice(h * BANK, (h + 1) * BANK)
+                if fp4:
+                    rhs = words[:, 2 * h * BANK : 2 * (h + 1) * BANK].bitcast(FP4X4)
+                else:
+                    rhs = words[:, cols].bitcast(FP8X4)
+                nc.tensor.matmul_mx(
+                    out=bank[:], lhsT=codes.bitcast(FP8X4), lhsT_scale=scales,
+                    rhs=rhs, rhs_scale=plane[:, cols], start=True, stop=True,
+                )
+                banks.append(bank)
+            return banks
+
+        arch_plane = spread_scales(arch_st, TOKENS, 64, 0)
+        c0_ps = score("c0_ps", s_codes, s_scales[:], arch_w, arch_plane, True)
+
+        qv_bf = sb.tile([P, ROWS, PACK], BF16, align_bytes=64, tag="qv_then_f1")
+        nc.scalar.copy(out=qv_bf[:], in_=qv_ps[:].rearrange("p t q -> p q t"))
+        draft_plane = spread_scales(draft_st, TOKENS, 0, 4)
+        cache_plane = spread_scales(cache_st, TOKENS, 0, 0)
+        q_codes = cache_st[:, TOKENS : TOKENS + PACK * ROWS]
+        q_scales = draft_st[:, TOKENS : TOKENS + ROWS]
+        nc.vector.quantize_mx(
+            out=q_codes.bitcast(FP8X4), scales=q_scales, in_=qv_bf[:].rearrange("p q t -> p (q t)")
+        )
+        f1a = sb.tile([P, TOKENS], F32, align_bytes=64, tag="qv_then_f1")
+        nc.gpsimd.memset(f1a[:], 0.0)
+        b_ps = score("b_ps", q_codes, q_scales, draft_w, draft_plane, False)
+        f1b = sb.tile([P, TOKENS], F32, align_bytes=64, tag="draft_then_f1")
+        nc.gpsimd.memset(f1b[:], 0.0)
+        a_ps = score("a_ps", q_codes, q_scales, cache_w, cache_plane, True)
+
+        b_sb = sb.tile([P, TOKENS], F32)
+        a_sb = sb.tile([P, TOKENS], F32)
+        nc.scalar.copy(out=b_sb[:, 0:BANK], in_=b_ps[0][:])
+        nc.vector.tensor_copy(out=b_sb[:, BANK:TOKENS], in_=b_ps[1][:])
+        nc.scalar.copy(out=a_sb[:, 0:BANK], in_=a_ps[0][:])
+        nc.vector.tensor_copy(out=a_sb[:, BANK:TOKENS], in_=a_ps[1][:])
+
+        lo, hi = slice(0, HALF), slice(HALF, SLOTS)
+        gb = sb.tile([P, SLOTS], F32)
+        nc.scalar.activation(gb[:, lo], b_sb[:].indirect(half("l2", 0)), COPY)
+        nc.vector.tensor_copy(gb[:, hi], b_sb[:].indirect(half("l2", 1)))
+
+        w = sb.tile([P, SLOTS], F32)
+        ga = sb.tile([P, HALF], F32)
+        quarter = sb.tile([P, SLOTS], F32)
+        bars = [sb.tile([P, 1], F32, name="bar" + str(h), tag="bar_then_f2" + str(h)) for h in range(2)]
+        nc.vector.tensor_tensor(w[:, lo], a_sb[:].indirect(half("l1", 0)), gb[:, lo], ALU.subtract)
+        nc.scalar.activation(ga[:], a_sb[:].indirect(half("l1", 1)), COPY)
+        nc.vector.tensor_tensor(w[:, hi], ga[:], gb[:, hi], ALU.subtract)
+        for h, cols in enumerate((lo, hi)):
+            nc.vector.tensor_scalar(
+                quarter[:, cols], w[:, cols], 0.25, None, ALU.mult, ALU.max, accum_out=bars[h][:]
+            )
+        v = sb.tile([P, SLOTS], F32)
+        FIRST = 128
+        for window, s0, s1 in ((f1a, 0, FIRST), (f1b, FIRST, SLOTS)):
+            nc.vector.tensor_scalar(v[:, s0:s1], w[:, s0:s1], bars[0][:], bars[1][:], ALU.max, ALU.max)
+            nc.scalar.activation(
+                window[:].indirect(lists["l3"][:, s0 // GROUP : s1 // GROUP]), v[:, s0:s1], COPY
+            )
+        f2 = []
+        for h in range(2):
+            f2.append(sb.tile([P, TOKENS], F32, name="f2" + str(h), tag="bar_then_f2" + str(h)))
+            nc.gpsimd.memset(f2[h][:], 0.0)
+
+        c1 = sb.tile([P, TOKENS], F32)
+        for h in range(2):
+            cols = slice(h * BANK, (h + 1) * BANK)
+            nc.vector.tensor_tensor(c1[:, cols], c0_ps[h][:], f1a[:, cols], ALU.add)
+        cc = sb.tile([P, TOKENS], F32)
+        nc.vector.tensor_tensor(cc[:], c1[:], f1b[:], ALU.add)
+        r = sb.tile([P, SLOTS], F32)
+        for h, cols in enumerate((lo, hi)):
+            nc.vector.tensor_tensor(r[:, cols], cc[:].indirect(half("l4", h)), w[:, cols], ALU.subtract)
+            nc.scalar.activation(f2[h][:].indirect(half("l5", h)), r[:, cols], COPY)
+
+        a1 = sb.tile([P, TOKENS], F32)
+        nc.vector.tensor_tensor(a1[:], a_sb[:], f2[0][:], ALU.subtract)
+        aa = sb.tile([P, TOKENS], F32)
+        nc.vector.tensor_tensor(aa[:], a1[:], f2[1][:], ALU.subtract)
+        left = sb.tile([P, SLOTS], F32)
+        y = sb.tile([P, SLOTS], F32)
+        nc.vector.tensor_copy(left[:, lo], aa[:].indirect(half("l6", 0)))
+        nc.scalar.activation(left[:, hi], aa[:].indirect(half("l6", 1)), COPY)
+        for cols, queue in ((lo, nc.sync), (hi, nc.scalar)):
+            nc.vector.tensor_tensor(y[:, cols], left[:, cols], gb[:, cols], ALU.max)
+            queue.dma_start(out=out[:, cols], in_=y[:, cols])

@@ -40,13 +40,12 @@ def tile_attend_overbar_sidethree_kernel(
             engine.memset(t[base : base + 64, :].bitcast(I32), 0)
             return t
 
-        def load_scales(queue, t, scales, base, first):
+        def load_scales(t, scales, base, first, b):
             rows = scales[0].bitcast(I32).rearrange("(a b j) n -> b j a n", a=2, b=2)
-            for b in range(2):
-                p0 = base + 32 * b + first
-                queue.dma_start(
-                    out=t[p0 : p0 + 4, :].bitcast(I32).rearrange("j (a n) -> j a n", a=2), in_=rows[b]
-                )
+            p0 = base + 32 * b + first
+            nc.sync.dma_start(
+                out=t[p0 : p0 + 4, :].bitcast(I32).rearrange("j (a n) -> j a n", a=2), in_=rows[b]
+            )
 
         def spread_scales(t, width, base, first):
             low, high = slice(0, width), slice(width, 2 * width)
@@ -56,11 +55,12 @@ def tile_attend_overbar_sidethree_kernel(
             nc.vector.tensor_copy(out=t[0:64, high].bitcast(I32), in_=t[64:128, low].bitcast(I32))
             return t[first:P, high]
 
-        arch_st = scale_tile(nc.vector, "arch_st", TOKENS, 64)
+        draft_st = scale_tile(nc.vector, "draft_st", TOKENS, 0)
+        cache_st = scale_tile(nc.vector, "cache_st", TOKENS, 64)
         wq_st = sb.tile([P, FEATURES], U8, align_bytes=64)
         nc.vector.memset(wq_st[:].bitcast(I32), 0)
-        draft_st = scale_tile(nc.gpsimd, "draft_st", TOKENS, 0)
-        cache_st = scale_tile(nc.gpsimd, "cache_st", TOKENS, 0)
+        arch_sc = sb.tile([P, TOKENS], U8, align_bytes=64)
+        nc.vector.memset(arch_sc[:].bitcast(I32), 0)
 
         wq_rows = sb.tile([4, 4, FEATURES // 4], I32)
         nc.sync.dma_start(out=wq_rows[:], in_=wq_scales[0].bitcast(I32).rearrange("(g j) n -> j g n", j=4))
@@ -68,19 +68,28 @@ def tile_attend_overbar_sidethree_kernel(
         nc.sync.dma_start(out=raw[:], in_=states.rearrange("(p j) q -> p j q", j=PACK))
         wq_raw = sb.tile([P, FEATURES], U32, align_bytes=64)
         nc.sync.dma_start(out=wq_raw[:].bitcast(I32), in_=wq_words[0].rearrange("p n t -> p (n t)").bitcast(I32))
-        load_scales(nc.sync, arch_st, arch_scales, 64, 0)
-        arch_w = sb.tile([P, 2 * TOKENS], U8, align_bytes=64)
-        nc.sync.dma_start(out=arch_w[:].bitcast(I32), in_=arch_words[0].bitcast(I32))
-        load_scales(nc.sync, draft_st, draft_scales, 0, 4)
+        for b in range(2):
+            load_scales(draft_st, draft_scales, 0, 4, b)
+            load_scales(cache_st, cache_scales, 64, 0, b)
         draft_w = sb.tile([P, TOKENS], U32, align_bytes=64, tag="draft_then_f1")
         nc.sync.dma_start(out=draft_w[:].bitcast(I32), in_=draft_words[0].rearrange("p n t -> p (n t)").bitcast(I32))
-        load_scales(nc.sync, cache_st, cache_scales, 0, 0)
         cache_w = sb.tile([P, 2 * TOKENS], U8, align_bytes=64)
         nc.sync.dma_start(out=cache_w[:].bitcast(I32), in_=cache_words[0].bitcast(I32))
         lists = {}
-        for name, src in (("l2", offs2), ("l1", offs), ("l3", offs3), ("l4", offs4), ("l5", offs5), ("l6", offs6)):
+
+        def load_list(name, src):
             lists[name] = sb.tile([P, SLOTS // GROUP], U16, name=name)
             nc.sync.dma_start(lists[name][:], src)
+
+        load_list("l2", offs2)
+        load_list("l1", offs)
+        arch_w = sb.tile([P, 2 * TOKENS], U8, align_bytes=64)
+        nc.sync.dma_start(out=arch_w[:].bitcast(I32), in_=arch_words[0].bitcast(I32))
+        arch_rows = arch_scales[0].bitcast(I32).rearrange("(g j) n -> j g n", j=4)
+        for j in range(4):
+            nc.sync.dma_start(out=arch_sc[j:P:32, :].bitcast(I32), in_=arch_rows[j])
+        for name, src in (("l3", offs3), ("l4", offs4), ("l5", offs5), ("l6", offs6)):
+            load_list(name, src)
 
         def half(name, h):
             k = HALF // GROUP
@@ -104,7 +113,8 @@ def tile_attend_overbar_sidethree_kernel(
         undealt = wq_raw[:].rearrange("p (m t) -> p m t", t=PACK)
         nc.scalar.copy(out=dealt[:, 0:48, :], in_=undealt[:, 0:48, :])
         nc.vector.tensor_copy(out=dealt[:, 48:P, :].bitcast(I32), in_=undealt[:, 48:P, :].bitcast(I32))
-        s_codes = wq_raw[:, FEATURES - ROWS : FEATURES]
+        s_words = sb.tile([P, ROWS], U32, align_bytes=64)
+        s_codes = s_words[:]
         s_scales = sb.tile([P, ROWS], U8, align_bytes=64)
         nc.vector.quantize_mx(
             out=s_codes.bitcast(FP8X4), scales=s_scales[:], in_=grouped[:].rearrange("p q t -> p (q t)")
@@ -117,47 +127,46 @@ def tile_attend_overbar_sidethree_kernel(
                 rhs=s_codes.bitcast(FP8X4), rhs_scale=s_scales[:], start=True, stop=True,
             )
 
-        def score(name, codes, scales, words, plane, fp4):
+        def score(name, tag, codes, scales, words, plane, fp4, edges):
             banks = []
-            for h in range(TOKENS // BANK):
-                bank = ps.tile([P, BANK], F32, name=name + str(h))
-                cols = slice(h * BANK, (h + 1) * BANK)
+            for c0, c1 in zip(edges[:-1], edges[1:]):
+                bank = ps.tile([P, c1 - c0], F32, name=name + str(c0), tag=tag + str(c0))
                 if fp4:
-                    rhs = words[:, 2 * h * BANK : 2 * (h + 1) * BANK].bitcast(FP4X4)
+                    rhs = words[:, 2 * c0 : 2 * c1].bitcast(FP4X4)
                 else:
-                    rhs = words[:, cols].bitcast(FP8X4)
+                    rhs = words[:, c0:c1].bitcast(FP8X4)
                 nc.tensor.matmul_mx(
                     out=bank[:], lhsT=codes.bitcast(FP8X4), lhsT_scale=scales,
-                    rhs=rhs, rhs_scale=plane[:, cols], start=True, stop=True,
+                    rhs=rhs, rhs_scale=plane[:, c0:c1], start=True, stop=True,
                 )
                 banks.append(bank)
             return banks
 
-        arch_plane = spread_scales(arch_st, TOKENS, 64, 0)
-        c0_ps = score("c0_ps", s_codes, s_scales[:], arch_w, arch_plane, True)
 
         qv_bf = sb.tile([P, ROWS, PACK], BF16, align_bytes=64, tag="qv_then_f1")
         nc.scalar.copy(out=qv_bf[:], in_=qv_ps[:].rearrange("p t q -> p q t"))
         draft_plane = spread_scales(draft_st, TOKENS, 0, 4)
-        cache_plane = spread_scales(cache_st, TOKENS, 0, 0)
-        q_codes = cache_st[:, TOKENS : TOKENS + PACK * ROWS]
+        cache_plane = spread_scales(cache_st, TOKENS, 64, 0)
+        q_codes = cache_st[:, 0 : PACK * ROWS]
         q_scales = draft_st[:, TOKENS : TOKENS + ROWS]
         nc.vector.quantize_mx(
             out=q_codes.bitcast(FP8X4), scales=q_scales, in_=qv_bf[:].rearrange("p q t -> p (q t)")
         )
         f1a = sb.tile([P, TOKENS], F32, align_bytes=64, tag="qv_then_f1")
         nc.gpsimd.memset(f1a[:], 0.0)
-        b_ps = score("b_ps", q_codes, q_scales, draft_w, draft_plane, False)
+        b_ps = score("b_ps", "b_ps", q_codes, q_scales, draft_w, draft_plane, False, (0, 512, 1024))
         f1b = sb.tile([P, TOKENS], F32, align_bytes=64, tag="draft_then_f1")
         nc.gpsimd.memset(f1b[:], 0.0)
-        a_ps = score("a_ps", q_codes, q_scales, cache_w, cache_plane, True)
+        a_ps = score("a_ps", "a_then_c0", q_codes, q_scales, cache_w, cache_plane, True, (0, 512, 768, 1024))
 
         b_sb = sb.tile([P, TOKENS], F32)
         a_sb = sb.tile([P, TOKENS], F32)
         nc.scalar.copy(out=b_sb[:, 0:BANK], in_=b_ps[0][:])
         nc.vector.tensor_copy(out=b_sb[:, BANK:TOKENS], in_=b_ps[1][:])
         nc.scalar.copy(out=a_sb[:, 0:BANK], in_=a_ps[0][:])
-        nc.vector.tensor_copy(out=a_sb[:, BANK:TOKENS], in_=a_ps[1][:])
+        nc.vector.tensor_copy(out=a_sb[:, 512:768], in_=a_ps[1][:])
+        nc.vector.tensor_copy(out=a_sb[:, 768:1024], in_=a_ps[2][:])
+        c0_ps = score("c0_ps", "a_then_c0", s_codes, s_scales[:], arch_w, arch_sc[:], True, (0, 512, 1024))
 
         lo, hi = slice(0, HALF), slice(HALF, SLOTS)
         gb = sb.tile([P, SLOTS], F32)
@@ -170,8 +179,11 @@ def tile_attend_overbar_sidethree_kernel(
         bars = [sb.tile([P, 1], F32, name="bar" + str(h), tag="bar_then_f2" + str(h)) for h in range(2)]
         nc.vector.tensor_tensor(w[:, lo], a_sb[:].indirect(half("l1", 0)), gb[:, lo], ALU.subtract)
         nc.scalar.activation(ga[:], a_sb[:].indirect(half("l1", 1)), COPY)
-        nc.vector.tensor_tensor(w[:, hi], ga[:], gb[:, hi], ALU.subtract)
-        for h, cols in enumerate((lo, hi)):
+        LEAD = 32
+        for s0, s1 in ((0, LEAD), (LEAD, HALF)):
+            cols = slice(HALF + s0, HALF + s1)
+            nc.vector.tensor_tensor(w[:, cols], ga[:, s0:s1], gb[:, cols], ALU.subtract)
+        for h, cols in enumerate((slice(0, HALF + LEAD), slice(HALF + LEAD, SLOTS))):
             nc.vector.tensor_scalar(
                 quarter[:, cols], w[:, cols], 0.25, None, ALU.mult, ALU.max, accum_out=bars[h][:]
             )

@@ -55,17 +55,16 @@ def tile_attend_overbar_sidethree_kernel(
             nc.vector.tensor_copy(out=t[0:64, high].bitcast(I32), in_=t[64:128, low].bitcast(I32))
             return t[first:P, high]
 
+        wq_st = scale_tile(nc.vector, "wq_st", FEATURES, 0)
         draft_st = scale_tile(nc.vector, "draft_st", TOKENS, 0)
         cache_st = scale_tile(nc.vector, "cache_st", TOKENS, 64)
-        wq_st = sb.tile([P, FEATURES], U8, align_bytes=64)
-        nc.vector.memset(wq_st[:].bitcast(I32), 0)
         arch_sc = sb.tile([P, TOKENS], U8, align_bytes=64)
         nc.vector.memset(arch_sc[:].bitcast(I32), 0)
 
-        wq_rows = sb.tile([4, 4, FEATURES // 4], I32)
-        nc.sync.dma_start(out=wq_rows[:], in_=wq_scales[0].bitcast(I32).rearrange("(g j) n -> j g n", j=4))
         raw = sb.tile([P, PACK, ROWS], F32)
         nc.sync.dma_start(out=raw[:], in_=states.rearrange("(p j) q -> p j q", j=PACK))
+        for b in range(2):
+            load_scales(wq_st, wq_scales, 0, 8, b)
         wq_raw = sb.tile([P, FEATURES], U32, align_bytes=64)
         nc.sync.dma_start(out=wq_raw[:].bitcast(I32), in_=wq_words[0].rearrange("p n t -> p (n t)").bitcast(I32))
         for b in range(2):
@@ -96,23 +95,22 @@ def tile_attend_overbar_sidethree_kernel(
             return lists[name][:, h * k : (h + 1) * k]
 
 
-        for g in range(4):
-            nc.vector.tensor_copy(out=wq_st[32 * g : 32 * g + 4, :].bitcast(I32), in_=wq_rows[:, g, :])
         grouped = sb.tile([P, ROWS, PACK], BF16, align_bytes=64)
-        wq_sc = sb.tile([P, PACK, P], U8, align_bytes=64)
-        nc.vector.tensor_copy(
-            out=wq_sc[:].rearrange("p t m -> p m t"),
-            in_=wq_st[:].rearrange("p (m t) -> p m t", t=PACK),
-        )
         woven = grouped[:].rearrange("p (c i) t -> p c t i", i=4)
         planes = raw[:].rearrange("p t (c i) -> p c t i", i=4)
         nc.vector.tensor_copy(out=woven[:, 0:16], in_=planes[:, 0:16])
         nc.scalar.copy(out=woven[:, 16:32], in_=planes[:, 16:32])
+        spread_scales(wq_st, FEATURES, 0, 8)
+        wq_sc = sb.tile([P, PACK, P], U8, align_bytes=64)
+        nc.vector.tensor_copy(
+            out=wq_sc[:].rearrange("p t m -> p m t"),
+            in_=wq_st[:, 0:FEATURES].rearrange("p (m t) -> p m t", t=PACK),
+        )
         wq_w = sb.tile([P, PACK, P], U32, align_bytes=64)
         dealt = wq_w[:].rearrange("p t m -> p m t")
         undealt = wq_raw[:].rearrange("p (m t) -> p m t", t=PACK)
-        nc.scalar.copy(out=dealt[:, 0:48, :], in_=undealt[:, 0:48, :])
-        nc.vector.tensor_copy(out=dealt[:, 48:P, :].bitcast(I32), in_=undealt[:, 48:P, :].bitcast(I32))
+        nc.scalar.copy(out=dealt[:, 0:64, :], in_=undealt[:, 0:64, :])
+        nc.vector.tensor_copy(out=dealt[:, 64:P, :].bitcast(I32), in_=undealt[:, 64:P, :].bitcast(I32))
         s_words = sb.tile([P, ROWS], U32, align_bytes=64)
         s_codes = s_words[:]
         s_scales = sb.tile([P, ROWS], U8, align_bytes=64)
@@ -123,7 +121,7 @@ def tile_attend_overbar_sidethree_kernel(
         qv_ps = ps.tile([P, PACK, ROWS], F32)
         for t in range(PACK):
             nc.tensor.matmul_mx(
-                out=qv_ps[:, t, :], lhsT=wq_w[:, t, :].bitcast(FP8X4), lhsT_scale=wq_sc[:, t, :],
+                out=qv_ps[:, t, :], lhsT=wq_w[:, t, :].bitcast(FP8X4), lhsT_scale=wq_sc[8:P, t, :],
                 rhs=s_codes.bitcast(FP8X4), rhs_scale=s_scales[:], start=True, stop=True,
             )
 

from contextlib import ExitStack

import concourse.mybir as mybir

F32 = mybir.dt.float32
BF16 = mybir.dt.bfloat16
I32 = mybir.dt.int32
U32 = mybir.dt.uint32
U16 = mybir.dt.uint16
U8 = mybir.dt.uint8
FP8X4 = mybir.dt.float8_e4m3fn_x4
FP4X4 = mybir.dt.float4_e2m1fn_x4
ALU = mybir.AluOpType
COPY = mybir.ActivationFunctionType.Copy

P = 128
PACK = 4
FEATURES = 512
ROWS = 128
TOKENS = 1024
SLOTS = 512
BANK = 512
HALF = SLOTS // 2
GROUP = 16

FLOPS = 2 * FEATURES * ROWS * (FEATURES + 3 * TOKENS)


def tile_attend_overbar_sidethree_kernel(
    tc, states, wq_words, wq_scales, cache_words, cache_scales, draft_words, draft_scales,
    arch_words, arch_scales, offs, offs2, offs3, offs4, offs5, offs6, out,
):
    nc = tc.nc
    with ExitStack() as ctx:
        sb = ctx.enter_context(tc.tile_pool(name="sb", bufs=1))
        ps = ctx.enter_context(tc.psum_pool(name="ps", bufs=1))

        def scale_tile(engine, name, width, base):
            t = sb.tile([P, 2 * width], U8, name=name, align_bytes=64)
            engine.memset(t[base : base + 64, :].bitcast(I32), 0)
            return t

        def load_scales(t, scales, base, first, b):
            rows = scales[0].bitcast(I32).rearrange("(a b j) n -> b j a n", a=2, b=2)
            p0 = base + 32 * b + first
            nc.sync.dma_start(
                out=t[p0 : p0 + 4, :].bitcast(I32).rearrange("j (a n) -> j a n", a=2), in_=rows[b]
            )

        def spread_scales(t, width, base, first):
            low, high = slice(0, width), slice(width, 2 * width)
            if base == 0:
                nc.vector.tensor_copy(out=t[64:128, low].bitcast(I32), in_=t[0:64, high].bitcast(I32))
                return t[first:P, low]
            nc.vector.tensor_copy(out=t[0:64, high].bitcast(I32), in_=t[64:128, low].bitcast(I32))
            return t[first:P, high]

        wq_st = scale_tile(nc.vector, "wq_st", FEATURES, 0)
        draft_st = scale_tile(nc.vector, "draft_st", TOKENS, 0)
        cache_st = scale_tile(nc.vector, "cache_st", TOKENS, 64)
        arch_sc = sb.tile([P, TOKENS], U8, align_bytes=64)
        nc.vector.memset(arch_sc[:].bitcast(I32), 0)

        raw = sb.tile([P, PACK, ROWS], F32)
        nc.sync.dma_start(out=raw[:], in_=states.rearrange("(p j) q -> p j q", j=PACK))
        for b in range(2):
            load_scales(wq_st, wq_scales, 0, 8, b)
        wq_raw = sb.tile([P, FEATURES], U32, align_bytes=64)
        nc.sync.dma_start(out=wq_raw[:].bitcast(I32), in_=wq_words[0].rearrange("p n t -> p (n t)").bitcast(I32))
        for b in range(2):
            load_scales(draft_st, draft_scales, 0, 4, b)
            load_scales(cache_st, cache_scales, 64, 0, b)
        draft_w = sb.tile([P, TOKENS], U32, align_bytes=64, tag="draft_then_f1")
        nc.sync.dma_start(out=draft_w[:].bitcast(I32), in_=draft_words[0].rearrange("p n t -> p (n t)").bitcast(I32))
        cache_w = sb.tile([P, 2 * TOKENS], U8, align_bytes=64)
        nc.sync.dma_start(out=cache_w[:].bitcast(I32), in_=cache_words[0].bitcast(I32))
        lists = {}

        def load_list(name, src):
            lists[name] = sb.tile([P, SLOTS // GROUP], U16, name=name)
            nc.sync.dma_start(lists[name][:], src)

        load_list("l2", offs2)
        load_list("l1", offs)
        arch_w = sb.tile([P, 2 * TOKENS], U8, align_bytes=64)
        nc.sync.dma_start(out=arch_w[:].bitcast(I32), in_=arch_words[0].bitcast(I32))
        arch_rows = arch_scales[0].bitcast(I32).rearrange("(g j) n -> j g n", j=4)
        for j in range(4):
            nc.sync.dma_start(out=arch_sc[j:P:32, :].bitcast(I32), in_=arch_rows[j])
        for name, src in (("l3", offs3), ("l4", offs4), ("l5", offs5), ("l6", offs6)):
            load_list(name, src)

        def half(name, h):
            k = HALF // GROUP
            return lists[name][:, h * k : (h + 1) * k]


        grouped = sb.tile([P, ROWS, PACK], BF16, align_bytes=64)
        woven = grouped[:].rearrange("p (c i) t -> p c t i", i=4)
        planes = raw[:].rearrange("p t (c i) -> p c t i", i=4)
        nc.vector.tensor_copy(out=woven[:, 0:16], in_=planes[:, 0:16])
        nc.scalar.copy(out=woven[:, 16:32], in_=planes[:, 16:32])
        spread_scales(wq_st, FEATURES, 0, 8)
        wq_sc = sb.tile([P, PACK, P], U8, align_bytes=64)
        nc.vector.tensor_copy(
            out=wq_sc[:].rearrange("p t m -> p m t"),
            in_=wq_st[:, 0:FEATURES].rearrange("p (m t) -> p m t", t=PACK),
        )
        wq_w = sb.tile([P, PACK, P], U32, align_bytes=64)
        dealt = wq_w[:].rearrange("p t m -> p m t")
        undealt = wq_raw[:].rearrange("p (m t) -> p m t", t=PACK)
        nc.scalar.copy(out=dealt[:, 0:64, :], in_=undealt[:, 0:64, :])
        nc.vector.tensor_copy(out=dealt[:, 64:P, :].bitcast(I32), in_=undealt[:, 64:P, :].bitcast(I32))
        s_words = sb.tile([P, ROWS], U32, align_bytes=64)
        s_codes = s_words[:]
        s_scales = sb.tile([P, ROWS], U8, align_bytes=64)
        nc.vector.quantize_mx(
            out=s_codes.bitcast(FP8X4), scales=s_scales[:], in_=grouped[:].rearrange("p q t -> p (q t)")
        )

        qv_ps = ps.tile([P, PACK, ROWS], F32)
        for t in range(PACK):
            nc.tensor.matmul_mx(
                out=qv_ps[:, t, :], lhsT=wq_w[:, t, :].bitcast(FP8X4), lhsT_scale=wq_sc[8:P, t, :],
                rhs=s_codes.bitcast(FP8X4), rhs_scale=s_scales[:], start=True, stop=True,
            )

        def score(name, tag, codes, scales, words, plane, fp4, edges):
            banks = []
            for c0, c1 in zip(edges[:-1], edges[1:]):
                bank = ps.tile([P, c1 - c0], F32, name=name + str(c0), tag=tag + str(c0))
                if fp4:
                    rhs = words[:, 2 * c0 : 2 * c1].bitcast(FP4X4)
                else:
                    rhs = words[:, c0:c1].bitcast(FP8X4)
                nc.tensor.matmul_mx(
                    out=bank[:], lhsT=codes.bitcast(FP8X4), lhsT_scale=scales,
                    rhs=rhs, rhs_scale=plane[:, c0:c1], start=True, stop=True,
                )
                banks.append(bank)
            return banks


        qv_bf = sb.tile([P, ROWS, PACK], BF16, align_bytes=64, tag="qv_then_f1")
        nc.scalar.copy(out=qv_bf[:], in_=qv_ps[:].rearrange("p t q -> p q t"))
        draft_plane = spread_scales(draft_st, TOKENS, 0, 4)
        cache_plane = spread_scales(cache_st, TOKENS, 64, 0)
        q_codes = cache_st[:, 0 : PACK * ROWS]
        q_scales = draft_st[:, TOKENS : TOKENS + ROWS]
        nc.vector.quantize_mx(
            out=q_codes.bitcast(FP8X4), scales=q_scales, in_=qv_bf[:].rearrange("p q t -> p (q t)")
        )
        f1a = sb.tile([P, TOKENS], F32, align_bytes=64, tag="qv_then_f1")
        nc.gpsimd.memset(f1a[:], 0.0)
        b_ps = score("b_ps", "b_ps", q_codes, q_scales, draft_w, draft_plane, False, (0, 512, 1024))
        f1b = sb.tile([P, TOKENS], F32, align_bytes=64, tag="draft_then_f1")
        nc.gpsimd.memset(f1b[:], 0.0)
        a_ps = score("a_ps", "a_then_c0", q_codes, q_scales, cache_w, cache_plane, True, (0, 512, 768, 1024))

        b_sb = sb.tile([P, TOKENS], F32)
        a_sb = sb.tile([P, TOKENS], F32)
        nc.scalar.copy(out=b_sb[:, 0:BANK], in_=b_ps[0][:])
        nc.vector.tensor_copy(out=b_sb[:, BANK:TOKENS], in_=b_ps[1][:])
        nc.scalar.copy(out=a_sb[:, 0:BANK], in_=a_ps[0][:])
        nc.vector.tensor_copy(out=a_sb[:, 512:768], in_=a_ps[1][:])
        nc.vector.tensor_copy(out=a_sb[:, 768:1024], in_=a_ps[2][:])
        c0_ps = score("c0_ps", "a_then_c0", s_codes, s_scales[:], arch_w, arch_sc[:], True, (0, 512, 1024))

        lo, hi = slice(0, HALF), slice(HALF, SLOTS)
        gb = sb.tile([P, SLOTS], F32)
        nc.scalar.activation(gb[:, lo], b_sb[:].indirect(half("l2", 0)), COPY)
        nc.vector.tensor_copy(gb[:, hi], b_sb[:].indirect(half("l2", 1)))

        w = sb.tile([P, SLOTS], F32)
        ga = sb.tile([P, HALF], F32)
        quarter = sb.tile([P, SLOTS], F32)
        bars = [sb.tile([P, 1], F32, name="bar" + str(h), tag="bar_then_f2" + str(h)) for h in range(2)]
        nc.vector.tensor_tensor(w[:, lo], a_sb[:].indirect(half("l1", 0)), gb[:, lo], ALU.subtract)
        nc.scalar.activation(ga[:], a_sb[:].indirect(half("l1", 1)), COPY)
        LEAD = 32
        for s0, s1 in ((0, LEAD), (LEAD, HALF)):
            cols = slice(HALF + s0, HALF + s1)
            nc.vector.tensor_tensor(w[:, cols], ga[:, s0:s1], gb[:, cols], ALU.subtract)
        for h, cols in enumerate((slice(0, HALF + LEAD), slice(HALF + LEAD, SLOTS))):
            nc.vector.tensor_scalar(
                quarter[:, cols], w[:, cols], 0.25, None, ALU.mult, ALU.max, accum_out=bars[h][:]
            )
        v = sb.tile([P, SLOTS], F32)
        FIRST = 128
        for window, s0, s1 in ((f1a, 0, FIRST), (f1b, FIRST, SLOTS)):
            nc.vector.tensor_scalar(v[:, s0:s1], w[:, s0:s1], bars[0][:], bars[1][:], ALU.max, ALU.max)
            nc.scalar.activation(
                window[:].indirect(lists["l3"][:, s0 // GROUP : s1 // GROUP]), v[:, s0:s1], COPY
            )
        f2 = []
        for h in range(2):
            f2.append(sb.tile([P, TOKENS], F32, name="f2" + str(h), tag="bar_then_f2" + str(h)))
            nc.gpsimd.memset(f2[h][:], 0.0)

        c1 = sb.tile([P, TOKENS], F32)
        for h in range(2):
            cols = slice(h * BANK, (h + 1) * BANK)
            nc.vector.tensor_tensor(c1[:, cols], c0_ps[h][:], f1a[:, cols], ALU.add)
        cc = sb.tile([P, TOKENS], F32)
        nc.vector.tensor_tensor(cc[:], c1[:], f1b[:], ALU.add)
        r = sb.tile([P, SLOTS], F32)
        for h, cols in enumerate((lo, hi)):
            nc.vector.tensor_tensor(r[:, cols], cc[:].indirect(half("l4", h)), w[:, cols], ALU.subtract)
            nc.scalar.activation(f2[h][:].indirect(half("l5", h)), r[:, cols], COPY)

        a1 = sb.tile([P, TOKENS], F32)
        nc.vector.tensor_tensor(a1[:], a_sb[:], f2[0][:], ALU.subtract)
        aa = sb.tile([P, TOKENS], F32)
        nc.vector.tensor_tensor(aa[:], a1[:], f2[1][:], ALU.subtract)
        left = sb.tile([P, SLOTS], F32)
        y = sb.tile([P, SLOTS], F32)
        nc.vector.tensor_copy(left[:, lo], aa[:].indirect(half("l6", 0)))
        nc.scalar.activation(left[:, hi], aa[:].indirect(half("l6", 1)), COPY)
        for cols, queue in ((lo, nc.sync), (hi, nc.scalar)):
            nc.vector.tensor_tensor(y[:, cols], left[:, cols], gb[:, cols], ALU.max)
            queue.dma_start(out=out[:, cols], in_=y[:, cols])
